import numpy as np
import ml_dtypes


def mxq(x, axis, fmt="e4m3"):
    dtype, down = {"e4m3": (ml_dtypes.float8_e4m3fn, 7), "e5m2": (ml_dtypes.float8_e5m2, 14)}[fmt]
    v = np.moveaxis(np.asarray(x, np.float32).astype(ml_dtypes.bfloat16).astype(np.float64), axis, -1)
    blocks = v.reshape(v.shape[:-1] + (-1, 32))
    amax = np.abs(blocks).max(-1, keepdims=True)
    byte = np.maximum(np.where(amax > 0, np.frexp(amax)[1] - 1 + 127, 0) - down, 1)
    scale = np.exp2(byte - 127.0)
    codes = (blocks / scale).astype(np.float32).astype(dtype).astype(np.float64)
    return np.moveaxis((codes * scale).reshape(v.shape), -1, axis)


WIDE = False


def mx_kscale(k):
    if not WIDE:
        return np.ones(k)
    levels = np.array([10, -10, 5, -5, 0])
    if k % 512:
        return np.exp2(np.random.permutation(np.resize(levels, k // 32))).repeat(32)
    a = np.empty((k // 512, 16))
    for p in range(k // 512):
        a[p, :8] = np.random.permutation(np.resize(levels, 8))
        for g in range(8):
            far = levels[np.abs(levels - a[p, g]) >= 10]
            a[p, g + 8] = far[np.random.randint(len(far))]
    return np.exp2(a.ravel()).repeat(32)


def f64(x):
    return np.asarray(x).astype(np.float64)


def striped(idx):
    return np.tile(idx.reshape(-1, 16).T, (8, 1)).astype(np.uint16)


def unstriped(offs):
    return offs[:16].T.reshape(-1).astype(np.int64)


E2M1 = np.array([0.0, 0.5, 1.0, 1.5, 2.0, 3.0, 4.0, 6.0, -0.0, -0.5, -1.0, -1.5, -2.0, -3.0, -4.0, -6.0])


def pack_weight(w, fmt):
    k, n = w.shape
    w = f64(np.asarray(w, np.float32).astype(ml_dtypes.bfloat16)).reshape(k // 32, 32, n)
    amax = np.abs(w).max(1)
    if fmt == "e4m3":
        byte = np.frexp(amax)[1] - 1 + 127 - 7
    else:
        mant, ex = np.frexp(amax / 6.0)
        byte = np.where(mant > 0.5, ex, ex - 1) + 127
    byte = np.clip(np.where(amax > 0, byte, 1), 1, 254)
    scaled = (w * np.exp2(127.0 - byte)[:, None, :]).reshape(k, n).astype(np.float32)
    by_word = np.ascontiguousarray(scaled.reshape(k // 512, 128, 4, n).transpose(0, 1, 3, 2))
    if fmt == "e4m3":
        words = by_word.astype(ml_dtypes.float8_e4m3fn).view(np.uint8)
    else:
        c = by_word.astype(ml_dtypes.float4_e2m1fn).view(np.uint8) & 0xF
        words = (c[..., 0::2] | (c[..., 1::2] << 4)).reshape(k // 512, 128, 2 * n)
    return np.ascontiguousarray(words), np.ascontiguousarray(byte.astype(np.uint8).reshape(k // 512, 16, n))


def unpack_weight(words, scales, fmt):
    g, _, n = scales.shape
    words = np.ascontiguousarray(words).reshape(g, 128, n, -1)
    if fmt == "e4m3":
        vals = words.view(ml_dtypes.float8_e4m3fn).astype(np.float64)
    else:
        nib = np.empty((g, 128, n, 4), np.uint8)
        nib[..., 0::2] = words & 0xF
        nib[..., 1::2] = words >> 4
        vals = E2M1[nib]
    vals = vals * np.repeat(np.exp2(scales.astype(np.float64) - 127.0), 8, axis=1)[..., None]
    return vals.transpose(0, 1, 3, 2).reshape(g * 512, n)


def gelu(v):
    return 0.5 * v * (1.0 + np.tanh(np.sqrt(2.0 / np.pi) * (v + 0.044715 * v**3)))


K, T, S, H, P, P2, N = 1024, 4096, 1024, 512, 512, 256, 768

def setup_inputs():
    n = np.random.standard_normal
    s = mx_kscale(K)[:, None]
    u = mx_kscale(H)[:, None]
    tab_words, tab_scales = pack_weight(n((K, T)) * s, "e4m3")
    w2_words, w2_scales = pack_weight(1.4 * n((K, H)) / np.sqrt(K) / s, "e2m1")
    w5_words, w5_scales = pack_weight(1.3 * n((H, N)) / np.sqrt(H) / u, "e2m1")
    return {
        "tab_words": tab_words, "tab_scales": tab_scales,
        "offs": striped(np.random.permutation(T)[:S]),
        "pos1": striped(np.random.permutation(S)[:P]),
        "pos2": striped(np.random.permutation(S)[:P]),
        "pos3": striped(np.random.permutation(P)[:P2]),
        "pos4": striped(np.random.permutation(S)[:P2]),
        "w1": (1.2 * n((K, H)) / np.sqrt(K) / s * u.T).astype(np.float32),
        "w2_words": w2_words, "w2_scales": w2_scales,
        "w3": (0.9 * n((K, H)) / np.sqrt(K) / s * u.T).astype(np.float32),
        "w4": (2.5 * n((H, N)) / np.sqrt(H) / u).astype(np.float32),
        "w5_words": w5_words, "w5_scales": w5_scales,
    }

def reference(tab_words, tab_scales, offs, pos1, pos2, pos3, pos4, w1, w2_words, w2_scales, w3, w4, w5_words, w5_scales):
    v = unpack_weight(tab_words, tab_scales, "e4m3")[:, unstriped(offs)]
    w2 = unpack_weight(w2_words, w2_scales, "e2m1")
    w5 = unpack_weight(w5_words, w5_scales, "e2m1")
    value = mxq(f64(w1), 0, "e4m3").T @ v
    turn = np.tanh(w2.T @ v)
    bound = mxq(f64(w3), 0, "e4m3").T @ v
    h = np.minimum(value * turn, bound)
    a1 = h[:, unstriped(pos1)] + h[:, unstriped(pos2)]
    a2 = np.maximum(a1[:, unstriped(pos3)], h[:, unstriped(pos4)])
    aq = mxq(a2, 0, "e4m3")
    bent = np.tanh(mxq(f64(w4), 0, "e4m3").T @ aq)
    straight = w5.T @ aq
    return bent + straight

@@ -1,0 +1,241 @@
+from contextlib import ExitStack
+
+import concourse.mybir as mybir
+
+K, T, S, H, PAIRS, KEPT, N = 1024, 4096, 1024, 512, 512, 256, 768
+FLOPS = 2 * (3 * K * H * S + 2 * H * N * KEPT)
+
+F32 = mybir.dt.float32
+BF16 = mybir.dt.bfloat16
+I32 = mybir.dt.int32
+U32 = mybir.dt.uint32
+U16 = mybir.dt.uint16
+U8 = mybir.dt.uint8
+E4M3 = mybir.dt.float8_e4m3fn_x4
+E2M1 = mybir.dt.float4_e2m1fn_x4
+ALU = mybir.AluOpType
+TANH = mybir.ActivationFunctionType.Tanh
+
+P = 128
+PACK = 4
+PASSES = K // (P * PACK)
+BANK = 512
+HALVES = S // BANK
+QUADS = 4
+
+
+def tile_list_delay_cause_features_kernel(
+    tc, tab_words, tab_scales, offs, pos1, pos2, pos3, pos4, w1, w2_words, w2_scales, w3, w4, w5_words, w5_scales, out
+):
+    nc = tc.nc
+    with ExitStack() as ctx:
+        keep = ctx.enter_context(tc.tile_pool(name="keep", bufs=1))
+        ring = ctx.enter_context(tc.tile_pool(name="ring", bufs=2))
+        psum = ctx.enter_context(tc.psum_pool(name="psum", bufs=8))
+
+        def held(shape, dtype, name):
+            return keep.tile(shape, dtype, name=name, align_bytes=64)
+
+        def load_list(src, name):
+            tile = held([P, src.shape[1]], U16, name)
+            nc.sync.dma_start(tile[:], src)
+            return tile
+
+        def load_rows(src, a, name):
+            tile = held([P, PACK, src.shape[1]], F32, name)
+            nc.sync.dma_start(tile[:], src[a * P * PACK : (a + 1) * P * PACK, :].rearrange("(p j) c -> p j c", j=PACK))
+            return tile
+
+        tab_rows = held([P, T], U8, "tab_rows")
+        nc.vector.memset(tab_rows[:].bitcast(I32), 0)
+        w2_plane_raw = held([P, PASSES, H], U8, "w2_plane_raw")
+        nc.vector.memset(w2_plane_raw[:].bitcast(I32), 0)
+        lowered = held([P, S], U8, "lowered")
+        nc.vector.memset(lowered[:].bitcast(I32), 0)
+        w5_plane = held([P, N], U8, "w5_plane")
+        nc.vector.memset(w5_plane[:].bitcast(I32), 0)
+
+        offs_t = load_list(offs, "offs_t")
+        for q in range(QUADS):
+            nc.gpsimd.dma_start(
+                tab_rows[32 * q : 32 * q + 8, :].bitcast(I32), tab_scales[:, 4 * q : 4 * q + 4, :].bitcast(I32)
+            )
+        tab = [held([P, T], U32, f"tab{a}") for a in range(PASSES)]
+        nc.sync.dma_start(tab[0][:].bitcast(I32), tab_words[0].rearrange("p t i -> p (t i)").bitcast(I32))
+        w2_raw = held([P, PASSES, 2 * H], U8, "w2_raw")
+        nc.sync.dma_start(w2_raw[:].bitcast(I32), w2_words.rearrange("a p c -> p a c").bitcast(I32))
+        nc.sync.dma_start(tab[1][:].bitcast(I32), tab_words[1].rearrange("p t i -> p (t i)").bitcast(I32))
+        w1_raw = [load_rows(w1, a, f"w1_raw{a}") for a in range(PASSES)]
+        w3_raw = [load_rows(w3, a, f"w3_raw{a}") for a in range(PASSES)]
+        pos1_t = load_list(pos1, "pos1_t")
+        pos2_t = load_list(pos2, "pos2_t")
+        pos3_t = load_list(pos3, "pos3_t")
+        pos4_t = load_list(pos4, "pos4_t")
+        w4_raw = load_rows(w4, 0, "w4_raw")
+        w5_codes = held([P, 2 * N], U8, "w5_codes")
+        nc.sync.dma_start(w5_codes[:].bitcast(I32), w5_words[0].bitcast(I32))
+        for q in range(QUADS):
+            nc.sync.dma_start(
+                w5_plane[32 * q : 32 * q + 4, :].bitcast(I32), w5_scales[0, 4 * q : 4 * q + 4, :].bitcast(I32)
+            )
+        for q in range(QUADS):
+            nc.gpsimd.dma_start(
+                w2_plane_raw[32 * q : 32 * q + 4, :, :].bitcast(I32),
+                w2_scales[:, 4 * q : 4 * q + 4, :].rearrange("a r c -> r a c").bitcast(I32),
+            )
+
+        picked_rows = held([P, S], U8, "picked_rows")
+        nc.vector.tensor_copy(picked_rows[:], tab_rows[:].indirect(offs_t[:]))
+        nc.gpsimd.dma_start(lowered[0:100, :].bitcast(I32), picked_rows[4:104, :].bitcast(I32))
+        v_plane = [picked_rows, lowered]
+
+        v_codes = held([P, PASSES, S], U32, "v_codes")
+        nc.vector.tensor_copy(v_codes[:, 0, :], tab[0][:].indirect(offs_t[:]))
+        w2_codes = held([P, PASSES, 2 * H], U8, "w2_codes")
+        w2_plane = held([P, PASSES, H], U8, "w2_plane")
+        for a in range(PASSES):
+            nc.vector.tensor_copy(
+                w2_codes[:, a, :].rearrange("p (t m b) -> p t m b", t=PACK, b=2),
+                w2_raw[:, a, :].rearrange("p (m t b) -> p t m b", t=PACK, b=2),
+            )
+        nc.vector.tensor_copy(
+            w2_plane[:].rearrange("p a (t m) -> p a t m", t=PACK),
+            w2_plane_raw[:].rearrange("p a (m t) -> p a t m", t=PACK),
+        )
+        cols16 = BANK // 16
+        for half in range(HALVES):
+            nc.vector.tensor_copy(
+                v_codes[:, 1, half * BANK : (half + 1) * BANK],
+                tab[1][:].indirect(offs_t[:, half * cols16 : (half + 1) * cols16]),
+            )
+
+        def first_stage(codes, plane, dtype, width, t, half):
+            acc = psum.tile([P, BANK], F32, name="acc")
+            cols = slice(half * BANK, (half + 1) * BANK)
+            for a in range(PASSES):
+                nc.tensor.matmul_mx(
+                    out=acc[:],
+                    lhsT=codes[:, a, width * P * t : width * P * (t + 1)].bitcast(dtype),
+                    lhsT_scale=plane[:, a, P * t : P * (t + 1)],
+                    rhs=v_codes[:, a, cols].bitcast(E4M3),
+                    rhs_scale=v_plane[a][:, cols],
+                    start=(a == 0),
+                    stop=(a == PASSES - 1),
+                )
+            return acc
+
+        h = [held([P, S], F32, f"h{t}") for t in range(PACK)]
+        for t in range(PACK):
+            for half in range(HALVES):
+                acc = first_stage(w2_codes, w2_plane, E2M1, 2, t, half)
+                nc.scalar.activation(h[t][:, half * BANK : (half + 1) * BANK], acc[:], TANH)
+
+        def round_pair(copy, raw, u, name):
+            grouped = held([P, 2 * P * PACK], BF16, name)
+            copy(
+                grouped[:].rearrange("p (t m j) -> p m j t", t=2, j=PACK),
+                raw[:].rearrange("p j (m t) -> p m j t", t=PACK)[:, :, :, 2 * u : 2 * u + 2],
+            )
+            return grouped
+
+        def quantize_pair(grouped, codes, plane, a, u):
+            cols = slice(2 * P * u, 2 * P * (u + 1))
+            nc.vector.quantize_mx(out=codes[:, a, cols].bitcast(E4M3), scales=plane[:, a, cols], in_=grouped[:])
+
+        w1_codes = held([P, PASSES, H], U32, "w1_codes")
+        w1_plane = held([P, PASSES, H], U8, "w1_plane")
+        for a in range(PASSES):
+            rounded = [round_pair(nc.vector.tensor_copy, w1_raw[a], u, f"w1_bf{a}{u}") for u in range(2)]
+            for u in range(2):
+                quantize_pair(rounded[u], w1_codes, w1_plane, a, u)
+
+        w3_codes = held([P, PASSES, H], U32, "w3_codes")
+        w3_plane = held([P, PASSES, H], U8, "w3_plane")
+        w3_rounded = {}
+        for u in range(2):
+            for a in range(PASSES):
+                w3_rounded[a, u] = round_pair(nc.scalar.copy, w3_raw[a], u, f"w3_bf{a}{u}")
+
+        for t in range(PACK):
+            for half in range(HALVES):
+                acc = first_stage(w1_codes, w1_plane, E4M3, 1, t, half)
+                part = h[t][:, half * BANK : (half + 1) * BANK]
+                nc.vector.tensor_tensor(part, acc[:], part, ALU.mult)
+            if t >= 2:
+                quantize_pair(w3_rounded[t - 2, 0], w3_codes, w3_plane, t - 2, 0)
+
+        w4_bf = held([P, N * PACK], BF16, "w4_bf")
+        nc.scalar.copy(
+            w4_bf[:].rearrange("p (c i j) -> p c j i", i=4, j=PACK),
+            w4_raw[:].rearrange("p j (c i) -> p c j i", i=4),
+        )
+        w4_codes = held([P, N], U32, "w4_codes")
+        w4_plane = held([P, N], U8, "w4_plane")
+
+        def bound(t):
+            for half in range(HALVES):
+                acc = first_stage(w3_codes, w3_plane, E4M3, 1, t, half)
+                part = h[t][:, half * BANK : (half + 1) * BANK]
+                nc.vector.tensor_tensor(part, acc[:], part, ALU.min)
+
+        a2 = held([P, PACK, KEPT], F32, "a2")
+        bound(0)
+        for t in range(PACK):
+            first = ring.tile([P, PAIRS], F32, name="first")
+            nc.vector.tensor_copy(first[:], h[t][:].indirect(pos1_t[:]))
+            notice = ring.tile([P, KEPT], F32, name="notice")
+            nc.vector.tensor_copy(notice[:], h[t][:].indirect(pos4_t[:]))
+            a1 = ring.tile([P, PAIRS], F32, name="a1")
+            nc.vector.tensor_tensor(a1[:], h[t][:].indirect(pos2_t[:]), first[:], ALU.add)
+            if t == 0:
+                for a in range(PASSES):
+                    quantize_pair(w3_rounded[a, 1], w3_codes, w3_plane, a, 1)
+            if t == 1:
+                for u in range(2):
+                    cols = slice(u * N // 2, (u + 1) * N // 2)
+                    nc.vector.quantize_mx(
+                        out=w4_codes[:, cols].bitcast(E4M3),
+                        scales=w4_plane[:, cols],
+                        in_=w4_bf[:, u * N * 2 : (u + 1) * N * 2],
+                    )
+            if t + 1 < PACK:
+                bound(t + 1)
+            kept = ring.tile([P, KEPT], F32, name="kept")
+            nc.vector.tensor_copy(kept[:], a1[:].indirect(pos3_t[:]))
+            nc.vector.tensor_tensor(a2[:, t, :], kept[:], notice[:], ALU.max)
+
+        a2_bf = held([P, KEPT * PACK], BF16, "a2_bf")
+        nc.vector.tensor_copy(
+            a2_bf[:].rearrange("p (c i t) -> p c t i", i=4, t=PACK),
+            a2[:].rearrange("p t (c i) -> p c t i", i=4),
+        )
+        a2_codes = held([P, KEPT], U32, "a2_codes")
+        a2_plane = held([P, KEPT], U8, "a2_plane")
+        nc.vector.quantize_mx(out=a2_codes[:].bitcast(E4M3), scales=a2_plane[:], in_=a2_bf[:])
+
+        per_bank = BANK // KEPT
+        for b in range(N // P // per_bank):
+            bent = psum.tile([P, BANK], F32, name="acc")
+            straight = psum.tile([P, BANK], F32, name="acc")
+            for acc, codes, plane, dtype, width in (
+                (bent, w4_codes, w4_plane, E4M3, 1),
+                (straight, w5_codes, w5_plane, E2M1, 2),
+            ):
+                for i in range(per_bank):
+                    n = b * per_bank + i
+                    nc.tensor.matmul_mx(
+                        out=acc[:, i * KEPT : (i + 1) * KEPT],
+                        lhsT=codes[:, width * P * n : width * P * (n + 1)].bitcast(dtype),
+                        lhsT_scale=plane[:, P * n : P * (n + 1)],
+                        rhs=a2_codes[:].bitcast(E4M3),
+                        rhs_scale=a2_plane[:],
+                        start=True,
+                        stop=True,
+                    )
+            result = held([P, BANK], F32, f"result{b}")
+            nc.scalar.activation(result[:], bent[:], TANH)
+            nc.vector.tensor_tensor(result[:], straight[:], result[:], ALU.add)
+            nc.sync.dma_start(
+                out[b * per_bank * P : (b + 1) * per_bank * P, :].rearrange("(i p) j -> p i j", p=P),
+                result[:].rearrange("p (i j) -> p i j", i=per_bank),
+            )

@@ -46,31 +46,40 @@ def tile_list_delay_cause_features_kernel(
             nc.sync.dma_start(tile[:], src[a * P * PACK : (a + 1) * P * PACK, :].rearrange("(p j) c -> p j c", j=PACK))
             return tile
 
-        tab_rows = held([P, T], U8, "tab_rows")
-        nc.vector.memset(tab_rows[:].bitcast(I32), 0)
         w2_plane_raw = held([P, PASSES, H], U8, "w2_plane_raw")
         nc.vector.memset(w2_plane_raw[:].bitcast(I32), 0)
-        lowered = held([P, S], U8, "lowered")
-        nc.vector.memset(lowered[:].bitcast(I32), 0)
+        tab_rows = held([P, T], U8, "tab_rows")
+        nc.vector.memset(tab_rows[32:64, :].bitcast(I32), 0)
+        nc.vector.memset(tab_rows[64:128, :].bitcast(I32), 0)
+        v_plane = held([P, PASSES, S], U8, "v_plane")
+        nc.vector.memset(v_plane[:].bitcast(I32), 0)
         w5_plane = held([P, N], U8, "w5_plane")
         nc.vector.memset(w5_plane[:].bitcast(I32), 0)
 
         offs_t = load_list(offs, "offs_t")
-        for q in range(QUADS):
-            nc.gpsimd.dma_start(
-                tab_rows[32 * q : 32 * q + 8, :].bitcast(I32), tab_scales[:, 4 * q : 4 * q + 4, :].bitcast(I32)
-            )
+        nc.sync.dma_start(tab_rows[0:32, :].bitcast(I32), tab_scales.rearrange("a q t -> q a t").bitcast(I32))
         tab = [held([P, T], U32, f"tab{a}") for a in range(PASSES)]
         nc.sync.dma_start(tab[0][:].bitcast(I32), tab_words[0].rearrange("p t i -> p (t i)").bitcast(I32))
+        for q in range(QUADS):
+            nc.sync.dma_start(
+                w2_plane_raw[32 * q : 32 * q + 4, :, :].bitcast(I32),
+                w2_scales[:, 4 * q : 4 * q + 4, :].rearrange("a r c -> r a c").bitcast(I32),
+            )
         w2_raw = held([P, PASSES, 2 * H], U8, "w2_raw")
         nc.sync.dma_start(w2_raw[:].bitcast(I32), w2_words.rearrange("a p c -> p a c").bitcast(I32))
         nc.sync.dma_start(tab[1][:].bitcast(I32), tab_words[1].rearrange("p t i -> p (t i)").bitcast(I32))
+        picked_rows = held([P, S], U8, "picked_rows")
+        nc.vector.tensor_copy(picked_rows[:], tab_rows[:].indirect(offs_t[:]))
+        for q in range(QUADS):
+            nc.sync.dma_start(
+                v_plane[32 * q : 32 * q + 4, :, :].bitcast(I32), picked_rows[8 * q : 8 * q + 8, :].bitcast(I32)
+            )
         w1_raw = [load_rows(w1, a, f"w1_raw{a}") for a in range(PASSES)]
         w3_raw = [load_rows(w3, a, f"w3_raw{a}") for a in range(PASSES)]
         pos1_t = load_list(pos1, "pos1_t")
+        pos4_t = load_list(pos4, "pos4_t")
         pos2_t = load_list(pos2, "pos2_t")
         pos3_t = load_list(pos3, "pos3_t")
-        pos4_t = load_list(pos4, "pos4_t")
         w4_raw = load_rows(w4, 0, "w4_raw")
         w5_codes = held([P, 2 * N], U8, "w5_codes")
         nc.sync.dma_start(w5_codes[:].bitcast(I32), w5_words[0].bitcast(I32))
@@ -78,16 +87,6 @@ def tile_list_delay_cause_features_kernel(
             nc.sync.dma_start(
                 w5_plane[32 * q : 32 * q + 4, :].bitcast(I32), w5_scales[0, 4 * q : 4 * q + 4, :].bitcast(I32)
             )
-        for q in range(QUADS):
-            nc.gpsimd.dma_start(
-                w2_plane_raw[32 * q : 32 * q + 4, :, :].bitcast(I32),
-                w2_scales[:, 4 * q : 4 * q + 4, :].rearrange("a r c -> r a c").bitcast(I32),
-            )
-
-        picked_rows = held([P, S], U8, "picked_rows")
-        nc.vector.tensor_copy(picked_rows[:], tab_rows[:].indirect(offs_t[:]))
-        nc.gpsimd.dma_start(lowered[0:100, :].bitcast(I32), picked_rows[4:104, :].bitcast(I32))
-        v_plane = [picked_rows, lowered]
 
         v_codes = held([P, PASSES, S], U32, "v_codes")
         nc.vector.tensor_copy(v_codes[:, 0, :], tab[0][:].indirect(offs_t[:]))
@@ -118,7 +117,7 @@ def tile_list_delay_cause_features_kernel(
                     lhsT=codes[:, a, width * P * t : width * P * (t + 1)].bitcast(dtype),
                     lhsT_scale=plane[:, a, P * t : P * (t + 1)],
                     rhs=v_codes[:, a, cols].bitcast(E4M3),
-                    rhs_scale=v_plane[a][:, cols],
+                    rhs_scale=v_plane[:, a, cols],
                     start=(a == 0),
                     stop=(a == PASSES - 1),
                 )
@@ -145,7 +144,8 @@ def tile_list_delay_cause_features_kernel(
         w1_codes = held([P, PASSES, H], U32, "w1_codes")
         w1_plane = held([P, PASSES, H], U8, "w1_plane")
         for a in range(PASSES):
-            rounded = [round_pair(nc.vector.tensor_copy, w1_raw[a], u, f"w1_bf{a}{u}") for u in range(2)]
+            copies = (nc.vector.tensor_copy, nc.scalar.copy if a == PASSES - 1 else nc.vector.tensor_copy)
+            rounded = [round_pair(copies[u], w1_raw[a], u, f"w1_bf{a}{u}") for u in range(2)]
             for u in range(2):
                 quantize_pair(rounded[u], w1_codes, w1_plane, a, u)
 
@@ -178,13 +178,13 @@ def tile_list_delay_cause_features_kernel(
                 part = h[t][:, half * BANK : (half + 1) * BANK]
                 nc.vector.tensor_tensor(part, acc[:], part, ALU.min)
 
-        a2 = held([P, PACK, KEPT], F32, "a2")
+        kept = held([P, PACK, KEPT], F32, "kept")
+        notice = held([P, PACK, KEPT], F32, "notice")
         bound(0)
         for t in range(PACK):
             first = ring.tile([P, PAIRS], F32, name="first")
             nc.vector.tensor_copy(first[:], h[t][:].indirect(pos1_t[:]))
-            notice = ring.tile([P, KEPT], F32, name="notice")
-            nc.vector.tensor_copy(notice[:], h[t][:].indirect(pos4_t[:]))
+            nc.vector.tensor_copy(notice[:, t, :], h[t][:].indirect(pos4_t[:]))
             a1 = ring.tile([P, PAIRS], F32, name="a1")
             nc.vector.tensor_tensor(a1[:], h[t][:].indirect(pos2_t[:]), first[:], ALU.add)
             if t == 0:
@@ -200,14 +200,14 @@ def tile_list_delay_cause_features_kernel(
                     )
             if t + 1 < PACK:
                 bound(t + 1)
-            kept = ring.tile([P, KEPT], F32, name="kept")
-            nc.vector.tensor_copy(kept[:], a1[:].indirect(pos3_t[:]))
-            nc.vector.tensor_tensor(a2[:, t, :], kept[:], notice[:], ALU.max)
+            nc.vector.tensor_copy(kept[:, t, :], a1[:].indirect(pos3_t[:]))
 
         a2_bf = held([P, KEPT * PACK], BF16, "a2_bf")
-        nc.vector.tensor_copy(
+        nc.vector.tensor_tensor(
             a2_bf[:].rearrange("p (c i t) -> p c t i", i=4, t=PACK),
-            a2[:].rearrange("p t (c i) -> p c t i", i=4),
+            kept[:].rearrange("p t (c i) -> p c t i", i=4),
+            notice[:].rearrange("p t (c i) -> p c t i", i=4),
+            ALU.max,
         )
         a2_codes = held([P, KEPT], U32, "a2_codes")
         a2_plane = held([P, KEPT], U8, "a2_plane")

@@ -1,6 +1,7 @@
 from contextlib import ExitStack
 
 import concourse.mybir as mybir
+from concourse.masks import make_identity
 
 K, T, S, H, PAIRS, KEPT, N = 1024, 4096, 1024, 512, 512, 256, 768
 FLOPS = 2 * (3 * K * H * S + 2 * H * N * KEPT)
@@ -31,7 +32,8 @@ def tile_list_delay_cause_features_kernel(
     with ExitStack() as ctx:
         keep = ctx.enter_context(tc.tile_pool(name="keep", bufs=1))
         ring = ctx.enter_context(tc.tile_pool(name="ring", bufs=2))
-        psum = ctx.enter_context(tc.psum_pool(name="psum", bufs=8))
+        psum = ctx.enter_context(tc.psum_pool(name="psum", bufs=6))
+        psum_turn = ctx.enter_context(tc.psum_pool(name="psum_turn", bufs=1))
 
         def held(shape, dtype, name):
             return keep.tile(shape, dtype, name=name, align_bytes=64)
@@ -46,34 +48,42 @@ def tile_list_delay_cause_features_kernel(
             nc.sync.dma_start(tile[:], src[a * P * PACK : (a + 1) * P * PACK, :].rearrange("(p j) c -> p j c", j=PACK))
             return tile
 
-        w2_plane_raw = held([P, PASSES, H], U8, "w2_plane_raw")
-        nc.vector.memset(w2_plane_raw[:].bitcast(I32), 0)
         tab_rows = held([P, T], U8, "tab_rows")
-        nc.vector.memset(tab_rows[32:64, :].bitcast(I32), 0)
-        nc.vector.memset(tab_rows[64:128, :].bitcast(I32), 0)
-        v_plane = held([P, PASSES, S], U8, "v_plane")
-        nc.vector.memset(v_plane[:].bitcast(I32), 0)
+        w2_rows = held([P, H], U8, "w2_rows")
+        for rows in (tab_rows, w2_rows):
+            nc.vector.memset(rows[32:64, :].bitcast(I32), 0)
+            nc.vector.memset(rows[64:128, :].bitcast(I32), 0)
+        planes = held([P, PASSES, S + H], U8, "planes")
+        nc.gpsimd.memset(planes[:].bitcast(I32), 0)
         w5_plane = held([P, N], U8, "w5_plane")
-        nc.vector.memset(w5_plane[:].bitcast(I32), 0)
+        nc.gpsimd.memset(w5_plane[:].bitcast(I32), 0)
+        ident = held([P, P], F32, "ident")
+        make_identity(nc, ident[:])
 
         offs_t = load_list(offs, "offs_t")
         nc.sync.dma_start(tab_rows[0:32, :].bitcast(I32), tab_scales.rearrange("a q t -> q a t").bitcast(I32))
+        nc.sync.dma_start(w2_rows[0:32, :].bitcast(I32), w2_scales.rearrange("a q c -> q a c").bitcast(I32))
         tab = [held([P, T], U32, f"tab{a}") for a in range(PASSES)]
         nc.sync.dma_start(tab[0][:].bitcast(I32), tab_words[0].rearrange("p t i -> p (t i)").bitcast(I32))
-        for q in range(QUADS):
-            nc.sync.dma_start(
-                w2_plane_raw[32 * q : 32 * q + 4, :, :].bitcast(I32),
-                w2_scales[:, 4 * q : 4 * q + 4, :].rearrange("a r c -> r a c").bitcast(I32),
-            )
         w2_raw = held([P, PASSES, 2 * H], U8, "w2_raw")
         nc.sync.dma_start(w2_raw[:].bitcast(I32), w2_words.rearrange("a p c -> p a c").bitcast(I32))
-        nc.sync.dma_start(tab[1][:].bitcast(I32), tab_words[1].rearrange("p t i -> p (t i)").bitcast(I32))
+        tab1_words = tab_words[1].rearrange("p t i -> p (t i)").bitcast(I32)
+        nc.sync.dma_start(tab[1][:, 0 : T // 2].bitcast(I32), tab1_words[:, 0 : T // 2])
         picked_rows = held([P, S], U8, "picked_rows")
         nc.vector.tensor_copy(picked_rows[:], tab_rows[:].indirect(offs_t[:]))
+        joined_rows = held([P, S + H], U8, "joined_rows")
+        nc.vector.tensor_copy(
+            joined_rows[:, S:].rearrange("p (t m) -> p t m", t=PACK),
+            w2_rows[:].rearrange("p (m t) -> p t m", t=PACK),
+        )
+        nc.vector.tensor_copy(joined_rows[:, 0:S].bitcast(I32), picked_rows[:].bitcast(I32))
         for q in range(QUADS):
             nc.sync.dma_start(
-                v_plane[32 * q : 32 * q + 4, :, :].bitcast(I32), picked_rows[8 * q : 8 * q + 8, :].bitcast(I32)
+                planes[32 * q : 32 * q + 4, :, :].bitcast(I32), joined_rows[8 * q : 8 * q + 8, :].bitcast(I32)
             )
+        nc.sync.dma_start(tab[1][:, T // 2 :].bitcast(I32), tab1_words[:, T // 2 :])
+        v_plane = planes[:, :, 0:S]
+        w2_plane = planes[:, :, S:]
         w1_raw = [load_rows(w1, a, f"w1_raw{a}") for a in range(PASSES)]
         w3_raw = [load_rows(w3, a, f"w3_raw{a}") for a in range(PASSES)]
         pos1_t = load_list(pos1, "pos1_t")
@@ -91,16 +101,11 @@ def tile_list_delay_cause_features_kernel(
         v_codes = held([P, PASSES, S], U32, "v_codes")
         nc.vector.tensor_copy(v_codes[:, 0, :], tab[0][:].indirect(offs_t[:]))
         w2_codes = held([P, PASSES, 2 * H], U8, "w2_codes")
-        w2_plane = held([P, PASSES, H], U8, "w2_plane")
         for a in range(PASSES):
             nc.vector.tensor_copy(
                 w2_codes[:, a, :].rearrange("p (t m b) -> p t m b", t=PACK, b=2),
                 w2_raw[:, a, :].rearrange("p (m t b) -> p t m b", t=PACK, b=2),
             )
-        nc.vector.tensor_copy(
-            w2_plane[:].rearrange("p a (t m) -> p a t m", t=PACK),
-            w2_plane_raw[:].rearrange("p a (m t) -> p a t m", t=PACK),
-        )
         cols16 = BANK // 16
         for half in range(HALVES):
             nc.vector.tensor_copy(
@@ -108,26 +113,30 @@ def tile_list_delay_cause_features_kernel(
                 tab[1][:].indirect(offs_t[:, half * cols16 : (half + 1) * cols16]),
             )
 
-        def first_stage(codes, plane, dtype, width, t, half):
+        def first_stage(codes, plane, dtype, width, t, half, order):
             acc = psum.tile([P, BANK], F32, name="acc")
             cols = slice(half * BANK, (half + 1) * BANK)
-            for a in range(PASSES):
+            for a in order:
                 nc.tensor.matmul_mx(
                     out=acc[:],
                     lhsT=codes[:, a, width * P * t : width * P * (t + 1)].bitcast(dtype),
                     lhsT_scale=plane[:, a, P * t : P * (t + 1)],
                     rhs=v_codes[:, a, cols].bitcast(E4M3),
                     rhs_scale=v_plane[:, a, cols],
-                    start=(a == 0),
-                    stop=(a == PASSES - 1),
+                    start=(a == order[0]),
+                    stop=(a == order[-1]),
                 )
             return acc
 
         h = [held([P, S], F32, f"h{t}") for t in range(PACK)]
-        for t in range(PACK):
+
+        def turn(t):
             for half in range(HALVES):
-                acc = first_stage(w2_codes, w2_plane, E2M1, 2, t, half)
+                acc = first_stage(w2_codes, w2_plane, E2M1, 2, t, half, (0, 1))
                 nc.scalar.activation(h[t][:, half * BANK : (half + 1) * BANK], acc[:], TANH)
+
+        for t in range(PACK):
+            turn(t)
 
         def round_pair(copy, raw, u, name):
             grouped = held([P, 2 * P * PACK], BF16, name)
@@ -143,24 +152,29 @@ def tile_list_delay_cause_features_kernel(
 
         w1_codes = held([P, PASSES, H], U32, "w1_codes")
         w1_plane = held([P, PASSES, H], U8, "w1_plane")
+        w1_rounded = {}
         for a in range(PASSES):
-            copies = (nc.vector.tensor_copy, nc.scalar.copy if a == PASSES - 1 else nc.vector.tensor_copy)
-            rounded = [round_pair(copies[u], w1_raw[a], u, f"w1_bf{a}{u}") for u in range(2)]
             for u in range(2):
-                quantize_pair(rounded[u], w1_codes, w1_plane, a, u)
+                copy = nc.vector.tensor_copy
+                w1_rounded[a, u] = round_pair(copy, w1_raw[a], u, f"w1_bf{a}{u}")
+            quantize_pair(w1_rounded[a, 0], w1_codes, w1_plane, a, 0)
+            if a == 0:
+                quantize_pair(w1_rounded[a, 1], w1_codes, w1_plane, a, 1)
 
         w3_codes = held([P, PASSES, H], U32, "w3_codes")
         w3_plane = held([P, PASSES, H], U8, "w3_plane")
         w3_rounded = {}
-        for u in range(2):
-            for a in range(PASSES):
-                w3_rounded[a, u] = round_pair(nc.scalar.copy, w3_raw[a], u, f"w3_bf{a}{u}")
 
         for t in range(PACK):
             for half in range(HALVES):
-                acc = first_stage(w1_codes, w1_plane, E4M3, 1, t, half)
+                acc = first_stage(w1_codes, w1_plane, E4M3, 1, t, half, (1, 0))
                 part = h[t][:, half * BANK : (half + 1) * BANK]
                 nc.vector.tensor_tensor(part, acc[:], part, ALU.mult)
+            if t == 0:
+                for u in range(2):
+                    for a in range(PASSES):
+                        w3_rounded[a, u] = round_pair(nc.scalar.copy, w3_raw[a], u, f"w3_bf{a}{u}")
+                quantize_pair(w1_rounded[1, 1], w1_codes, w1_plane, 1, 1)
             if t >= 2:
                 quantize_pair(w3_rounded[t - 2, 0], w3_codes, w3_plane, t - 2, 0)
 
@@ -170,37 +184,65 @@ def tile_list_delay_cause_features_kernel(
             w4_raw[:].rearrange("p j (c i) -> p c j i", i=4),
         )
         w4_codes = held([P, N], U32, "w4_codes")
-        w4_plane = held([P, N], U8, "w4_plane")
 
         def bound(t):
             for half in range(HALVES):
-                acc = first_stage(w3_codes, w3_plane, E4M3, 1, t, half)
+                acc = first_stage(w3_codes, w3_plane, E4M3, 1, t, half, (1, 0))
                 part = h[t][:, half * BANK : (half + 1) * BANK]
                 nc.vector.tensor_tensor(part, acc[:], part, ALU.min)
 
         kept = held([P, PACK, KEPT], F32, "kept")
         notice = held([P, PACK, KEPT], F32, "notice")
+
+        def add_by_transposes(both, a1):
+            turned = psum_turn.tile([P, PAIRS], F32, name="turned")
+            for c in range(PAIRS // P):
+                cols = slice(c * P, (c + 1) * P)
+                for i in range(2):
+                    nc.tensor.matmul(
+                        turned[:, cols], both[:, i, cols], ident[:], start=(i == 0), stop=(i == 1), is_transpose=True
+                    )
+            sums = ring.tile([P, PAIRS], F32, name="sums")
+            nc.scalar.copy(sums[:], turned[:])
+            back = psum_turn.tile([P, PAIRS], F32, name="back")
+            for c in range(PAIRS // P):
+                cols = slice(c * P, (c + 1) * P)
+                nc.tensor.transpose(back[:, cols], sums[:, cols], ident[:])
+            nc.scalar.copy(a1[:], back[:])
+
+        def keep_pairs(t):
+            nc.vector.tensor_copy(kept[:, t, :], a1[t][:].indirect(pos3_t[:]))
+
+        a1 = [held([P, PAIRS], F32, f"a1_{t}") for t in range(PACK)]
+        last = PACK - 1
         bound(0)
-        for t in range(PACK):
-            first = ring.tile([P, PAIRS], F32, name="first")
-            nc.vector.tensor_copy(first[:], h[t][:].indirect(pos1_t[:]))
-            nc.vector.tensor_copy(notice[:, t, :], h[t][:].indirect(pos4_t[:]))
-            a1 = ring.tile([P, PAIRS], F32, name="a1")
-            nc.vector.tensor_tensor(a1[:], h[t][:].indirect(pos2_t[:]), first[:], ALU.add)
+        for t in range(last):
+            both = ring.tile([P, 2, PAIRS], F32, name="both")
+            nc.vector.tensor_copy(both[:, 0, :], h[t][:].indirect(pos1_t[:]))
+            nc.vector.tensor_copy(both[:, 1, :], h[t][:].indirect(pos2_t[:]))
+            add_by_transposes(both, a1[t])
             if t == 0:
                 for a in range(PASSES):
                     quantize_pair(w3_rounded[a, 1], w3_codes, w3_plane, a, 1)
-            if t == 1:
-                for u in range(2):
-                    cols = slice(u * N // 2, (u + 1) * N // 2)
-                    nc.vector.quantize_mx(
-                        out=w4_codes[:, cols].bitcast(E4M3),
-                        scales=w4_plane[:, cols],
-                        in_=w4_bf[:, u * N * 2 : (u + 1) * N * 2],
-                    )
-            if t + 1 < PACK:
-                bound(t + 1)
-            nc.vector.tensor_copy(kept[:, t, :], a1[:].indirect(pos3_t[:]))
+            bound(t + 1)
+            nc.vector.tensor_copy(notice[:, t, :], h[t][:].indirect(pos4_t[:]))
+            if t > 0:
+                keep_pairs(t - 1)
+
+        first = keep.tile([P, PAIRS], F32, name="first", tag="first", align_bytes=64)
+        nc.vector.tensor_copy(first[:], h[last][:].indirect(pos1_t[:]))
+        nc.vector.tensor_copy(notice[:, last, :], h[last][:].indirect(pos4_t[:]))
+        nc.vector.tensor_tensor(a1[last][:], h[last][:].indirect(pos2_t[:]), first[:], ALU.add)
+        w4_plane = keep.tile([P, N], U8, name="w4_plane", tag="first", align_bytes=64)
+        for u in range(2):
+            cols = slice(u * N // 2, (u + 1) * N // 2)
+            nc.vector.quantize_mx(
+                out=w4_codes[:, cols].bitcast(E4M3),
+                scales=w4_plane[:, cols],
+                in_=w4_bf[:, u * N * 2 : (u + 1) * N * 2],
+            )
+        keep_pairs(last - 1)
+        keep_pairs(last)
 
         a2_bf = held([P, KEPT * PACK], BF16, "a2_bf")
         nc.vector.tensor_tensor(

from contextlib import ExitStack

import concourse.mybir as mybir
from concourse.masks import make_identity

K, T, S, H, PAIRS, KEPT, N = 1024, 4096, 1024, 512, 512, 256, 768
FLOPS = 2 * (3 * K * H * S + 2 * H * N * KEPT)

F32 = mybir.dt.float32
BF16 = mybir.dt.bfloat16
I32 = mybir.dt.int32
U32 = mybir.dt.uint32
U16 = mybir.dt.uint16
U8 = mybir.dt.uint8
E4M3 = mybir.dt.float8_e4m3fn_x4
E2M1 = mybir.dt.float4_e2m1fn_x4
ALU = mybir.AluOpType
TANH = mybir.ActivationFunctionType.Tanh

P = 128
PACK = 4
PASSES = K // (P * PACK)
BANK = 512
HALVES = S // BANK
QUADS = 4


def tile_list_delay_cause_features_kernel(
    tc, tab_words, tab_scales, offs, pos1, pos2, pos3, pos4, w1, w2_words, w2_scales, w3, w4, w5_words, w5_scales, out
):
    nc = tc.nc
    with ExitStack() as ctx:
        keep = ctx.enter_context(tc.tile_pool(name="keep", bufs=1))
        ring = ctx.enter_context(tc.tile_pool(name="ring", bufs=2))
        psum = ctx.enter_context(tc.psum_pool(name="psum", bufs=6))
        psum_turn = ctx.enter_context(tc.psum_pool(name="psum_turn", bufs=1))

        def held(shape, dtype, name):
            return keep.tile(shape, dtype, name=name, align_bytes=64)

        def load_list(src, name):
            tile = held([P, src.shape[1]], U16, name)
            nc.sync.dma_start(tile[:], src)
            return tile

        def load_rows(src, a, name):
            tile = held([P, PACK, src.shape[1]], F32, name)
            nc.sync.dma_start(tile[:], src[a * P * PACK : (a + 1) * P * PACK, :].rearrange("(p j) c -> p j c", j=PACK))
            return tile

        tab_rows = held([P, T], U8, "tab_rows")
        w2_rows = held([P, H], U8, "w2_rows")
        for rows in (tab_rows, w2_rows):
            nc.vector.memset(rows[32:64, :].bitcast(I32), 0)
            nc.vector.memset(rows[64:128, :].bitcast(I32), 0)
        planes = held([P, PASSES, S + H], U8, "planes")
        nc.gpsimd.memset(planes[:].bitcast(I32), 0)
        w5_plane = held([P, N], U8, "w5_plane")
        nc.gpsimd.memset(w5_plane[:].bitcast(I32), 0)
        ident = held([P, P], F32, "ident")
        make_identity(nc, ident[:])

        offs_t = load_list(offs, "offs_t")
        nc.sync.dma_start(tab_rows[0:32, :].bitcast(I32), tab_scales.rearrange("a q t -> q a t").bitcast(I32))
        nc.sync.dma_start(w2_rows[0:32, :].bitcast(I32), w2_scales.rearrange("a q c -> q a c").bitcast(I32))
        tab = [held([P, T], U32, f"tab{a}") for a in range(PASSES)]
        nc.sync.dma_start(tab[0][:].bitcast(I32), tab_words[0].rearrange("p t i -> p (t i)").bitcast(I32))
        w2_raw = held([P, PASSES, 2 * H], U8, "w2_raw")
        nc.sync.dma_start(w2_raw[:].bitcast(I32), w2_words.rearrange("a p c -> p a c").bitcast(I32))
        tab1_words = tab_words[1].rearrange("p t i -> p (t i)").bitcast(I32)
        nc.sync.dma_start(tab[1][:, 0 : T // 2].bitcast(I32), tab1_words[:, 0 : T // 2])
        picked_rows = held([P, S], U8, "picked_rows")
        nc.vector.tensor_copy(picked_rows[:], tab_rows[:].indirect(offs_t[:]))
        joined_rows = held([P, S + H], U8, "joined_rows")
        nc.vector.tensor_copy(
            joined_rows[:, S:].rearrange("p (t m) -> p t m", t=PACK),
            w2_rows[:].rearrange("p (m t) -> p t m", t=PACK),
        )
        nc.vector.tensor_copy(joined_rows[:, 0:S].bitcast(I32), picked_rows[:].bitcast(I32))
        for q in range(QUADS):
            nc.sync.dma_start(
                planes[32 * q : 32 * q + 4, :, :].bitcast(I32), joined_rows[8 * q : 8 * q + 8, :].bitcast(I32)
            )
        nc.sync.dma_start(tab[1][:, T // 2 :].bitcast(I32), tab1_words[:, T // 2 :])
        v_plane = planes[:, :, 0:S]
        w2_plane = planes[:, :, S:]
        w1_raw = [load_rows(w1, a, f"w1_raw{a}") for a in range(PASSES)]
        w3_raw = [load_rows(w3, a, f"w3_raw{a}") for a in range(PASSES)]
        pos1_t = load_list(pos1, "pos1_t")
        pos4_t = load_list(pos4, "pos4_t")
        pos2_t = load_list(pos2, "pos2_t")
        pos3_t = load_list(pos3, "pos3_t")
        w4_raw = load_rows(w4, 0, "w4_raw")
        w5_codes = held([P, 2 * N], U8, "w5_codes")
        nc.sync.dma_start(w5_codes[:].bitcast(I32), w5_words[0].bitcast(I32))
        for q in range(QUADS):
            nc.sync.dma_start(
                w5_plane[32 * q : 32 * q + 4, :].bitcast(I32), w5_scales[0, 4 * q : 4 * q + 4, :].bitcast(I32)
            )

        v_codes = held([P, PASSES, S], U32, "v_codes")
        nc.vector.tensor_copy(v_codes[:, 0, :], tab[0][:].indirect(offs_t[:]))
        w2_codes = held([P, PASSES, 2 * H], U8, "w2_codes")
        for a in range(PASSES):
            nc.vector.tensor_copy(
                w2_codes[:, a, :].rearrange("p (t m b) -> p t m b", t=PACK, b=2),
                w2_raw[:, a, :].rearrange("p (m t b) -> p t m b", t=PACK, b=2),
            )
        cols16 = BANK // 16
        for half in range(HALVES):
            nc.vector.tensor_copy(
                v_codes[:, 1, half * BANK : (half + 1) * BANK],
                tab[1][:].indirect(offs_t[:, half * cols16 : (half + 1) * cols16]),
            )

        def first_stage(codes, plane, dtype, width, t, half, order):
            acc = psum.tile([P, BANK], F32, name="acc")
            cols = slice(half * BANK, (half + 1) * BANK)
            for a in order:
                nc.tensor.matmul_mx(
                    out=acc[:],
                    lhsT=codes[:, a, width * P * t : width * P * (t + 1)].bitcast(dtype),
                    lhsT_scale=plane[:, a, P * t : P * (t + 1)],
                    rhs=v_codes[:, a, cols].bitcast(E4M3),
                    rhs_scale=v_plane[:, a, cols],
                    start=(a == order[0]),
                    stop=(a == order[-1]),
                )
            return acc

        h = [held([P, S], F32, f"h{t}") for t in range(PACK)]

        def turn(t):
            for half in range(HALVES):
                acc = first_stage(w2_codes, w2_plane, E2M1, 2, t, half, (0, 1))
                nc.scalar.activation(h[t][:, half * BANK : (half + 1) * BANK], acc[:], TANH)

        for t in range(PACK):
            turn(t)

        def round_pair(copy, raw, u, name):
            grouped = held([P, 2 * P * PACK], BF16, name)
            copy(
                grouped[:].rearrange("p (t m j) -> p m j t", t=2, j=PACK),
                raw[:].rearrange("p j (m t) -> p m j t", t=PACK)[:, :, :, 2 * u : 2 * u + 2],
            )
            return grouped

        def quantize_pair(grouped, codes, plane, a, u):
            cols = slice(2 * P * u, 2 * P * (u + 1))
            nc.vector.quantize_mx(out=codes[:, a, cols].bitcast(E4M3), scales=plane[:, a, cols], in_=grouped[:])

        w1_codes = held([P, PASSES, H], U32, "w1_codes")
        w1_plane = held([P, PASSES, H], U8, "w1_plane")
        w1_rounded = {}
        for a in range(PASSES):
            for u in range(2):
                copy = nc.vector.tensor_copy
                w1_rounded[a, u] = round_pair(copy, w1_raw[a], u, f"w1_bf{a}{u}")
            quantize_pair(w1_rounded[a, 0], w1_codes, w1_plane, a, 0)
            if a == 0:
                quantize_pair(w1_rounded[a, 1], w1_codes, w1_plane, a, 1)

        w3_codes = held([P, PASSES, H], U32, "w3_codes")
        w3_plane = held([P, PASSES, H], U8, "w3_plane")
        w3_rounded = {}

        for t in range(PACK):
            for half in range(HALVES):
                acc = first_stage(w1_codes, w1_plane, E4M3, 1, t, half, (1, 0))
                part = h[t][:, half * BANK : (half + 1) * BANK]
                nc.vector.tensor_tensor(part, acc[:], part, ALU.mult)
            if t == 0:
                for u in range(2):
                    for a in range(PASSES):
                        w3_rounded[a, u] = round_pair(nc.scalar.copy, w3_raw[a], u, f"w3_bf{a}{u}")
                quantize_pair(w1_rounded[1, 1], w1_codes, w1_plane, 1, 1)
            if t >= 2:
                quantize_pair(w3_rounded[t - 2, 0], w3_codes, w3_plane, t - 2, 0)

        w4_bf = held([P, N * PACK], BF16, "w4_bf")
        nc.scalar.copy(
            w4_bf[:].rearrange("p (c i j) -> p c j i", i=4, j=PACK),
            w4_raw[:].rearrange("p j (c i) -> p c j i", i=4),
        )
        w4_codes = held([P, N], U32, "w4_codes")

        def bound(t):
            for half in range(HALVES):
                acc = first_stage(w3_codes, w3_plane, E4M3, 1, t, half, (1, 0))
                part = h[t][:, half * BANK : (half + 1) * BANK]
                nc.vector.tensor_tensor(part, acc[:], part, ALU.min)

        kept = held([P, PACK, KEPT], F32, "kept")
        notice = held([P, PACK, KEPT], F32, "notice")

        def add_by_transposes(both, a1):
            turned = psum_turn.tile([P, PAIRS], F32, name="turned")
            for c in range(PAIRS // P):
                cols = slice(c * P, (c + 1) * P)
                for i in range(2):
                    nc.tensor.matmul(
                        turned[:, cols], both[:, i, cols], ident[:], start=(i == 0), stop=(i == 1), is_transpose=True
                    )
            sums = ring.tile([P, PAIRS], F32, name="sums")
            nc.scalar.copy(sums[:], turned[:])
            back = psum_turn.tile([P, PAIRS], F32, name="back")
            for c in range(PAIRS // P):
                cols = slice(c * P, (c + 1) * P)
                nc.tensor.transpose(back[:, cols], sums[:, cols], ident[:])
            nc.scalar.copy(a1[:], back[:])

        def keep_pairs(t):
            nc.vector.tensor_copy(kept[:, t, :], a1[t][:].indirect(pos3_t[:]))

        a1 = [held([P, PAIRS], F32, f"a1_{t}") for t in range(PACK)]
        last = PACK - 1
        bound(0)
        for t in range(last):
            both = ring.tile([P, 2, PAIRS], F32, name="both")
            nc.vector.tensor_copy(both[:, 0, :], h[t][:].indirect(pos1_t[:]))
            nc.vector.tensor_copy(both[:, 1, :], h[t][:].indirect(pos2_t[:]))
            add_by_transposes(both, a1[t])
            if t == 0:
                for a in range(PASSES):
                    quantize_pair(w3_rounded[a, 1], w3_codes, w3_plane, a, 1)
            bound(t + 1)
            nc.vector.tensor_copy(notice[:, t, :], h[t][:].indirect(pos4_t[:]))
            if t > 0:
                keep_pairs(t - 1)

        first = keep.tile([P, PAIRS], F32, name="first", tag="first", align_bytes=64)
        nc.vector.tensor_copy(first[:], h[last][:].indirect(pos1_t[:]))
        nc.vector.tensor_copy(notice[:, last, :], h[last][:].indirect(pos4_t[:]))
        nc.vector.tensor_tensor(a1[last][:], h[last][:].indirect(pos2_t[:]), first[:], ALU.add)
        w4_plane = keep.tile([P, N], U8, name="w4_plane", tag="first", align_bytes=64)
        for u in range(2):
            cols = slice(u * N // 2, (u + 1) * N // 2)
            nc.vector.quantize_mx(
                out=w4_codes[:, cols].bitcast(E4M3),
                scales=w4_plane[:, cols],
                in_=w4_bf[:, u * N * 2 : (u + 1) * N * 2],
            )
        keep_pairs(last - 1)
        keep_pairs(last)

        a2_bf = held([P, KEPT * PACK], BF16, "a2_bf")
        nc.vector.tensor_tensor(
            a2_bf[:].rearrange("p (c i t) -> p c t i", i=4, t=PACK),
            kept[:].rearrange("p t (c i) -> p c t i", i=4),
            notice[:].rearrange("p t (c i) -> p c t i", i=4),
            ALU.max,
        )
        a2_codes = held([P, KEPT], U32, "a2_codes")
        a2_plane = held([P, KEPT], U8, "a2_plane")
        nc.vector.quantize_mx(out=a2_codes[:].bitcast(E4M3), scales=a2_plane[:], in_=a2_bf[:])

        per_bank = BANK // KEPT
        for b in range(N // P // per_bank):
            bent = psum.tile([P, BANK], F32, name="acc")
            straight = psum.tile([P, BANK], F32, name="acc")
            for acc, codes, plane, dtype, width in (
                (bent, w4_codes, w4_plane, E4M3, 1),
                (straight, w5_codes, w5_plane, E2M1, 2),
            ):
                for i in range(per_bank):
                    n = b * per_bank + i
                    nc.tensor.matmul_mx(
                        out=acc[:, i * KEPT : (i + 1) * KEPT],
                        lhsT=codes[:, width * P * n : width * P * (n + 1)].bitcast(dtype),
                        lhsT_scale=plane[:, P * n : P * (n + 1)],
                        rhs=a2_codes[:].bitcast(E4M3),
                        rhs_scale=a2_plane[:],
                        start=True,
                        stop=True,
                    )
            result = held([P, BANK], F32, f"result{b}")
            nc.scalar.activation(result[:], bent[:], TANH)
            nc.vector.tensor_tensor(result[:], straight[:], result[:], ALU.add)
            nc.sync.dma_start(
                out[b * per_bank * P : (b + 1) * per_bank * P, :].rearrange("(i p) j -> p i j", p=P),
                result[:].rearrange("p (i j) -> p i j", i=per_bank),
            )
